import numpy as np
import ml_dtypes


def mxq(x, axis, fmt="e4m3"):
    dtype, down = {"e4m3": (ml_dtypes.float8_e4m3fn, 7), "e5m2": (ml_dtypes.float8_e5m2, 14)}[fmt]
    v = np.moveaxis(np.asarray(x, np.float32).astype(ml_dtypes.bfloat16).astype(np.float64), axis, -1)
    blocks = v.reshape(v.shape[:-1] + (-1, 32))
    amax = np.abs(blocks).max(-1, keepdims=True)
    byte = np.maximum(np.where(amax > 0, np.frexp(amax)[1] - 1 + 127, 0) - down, 1)
    scale = np.exp2(byte - 127.0)
    codes = (blocks / scale).astype(np.float32).astype(dtype).astype(np.float64)
    return np.moveaxis((codes * scale).reshape(v.shape), -1, axis)


WIDE = False


def mx_kscale(k):
    if not WIDE:
        return np.ones(k)
    levels = np.array([30, -30])
    if k % 512:
        return np.exp2(np.random.permutation(np.resize(levels, k // 32))).repeat(32)
    a = np.empty((k // 512, 16))
    for p in range(k // 512):
        a[p, :8] = np.random.permutation(np.resize(levels, 8))
        for g in range(8):
            far = levels[np.abs(levels - a[p, g]) >= 10]
            a[p, g + 8] = far[np.random.randint(len(far))]
    return np.exp2(a.ravel()).repeat(32)


def f64(x):
    return np.asarray(x).astype(np.float64)


E2M1 = np.array([0.0, 0.5, 1.0, 1.5, 2.0, 3.0, 4.0, 6.0, -0.0, -0.5, -1.0, -1.5, -2.0, -3.0, -4.0, -6.0])


def pack_weight(w, fmt):
    k, n = w.shape
    w = f64(np.asarray(w, np.float32).astype(ml_dtypes.bfloat16)).reshape(k // 32, 32, n)
    amax = np.abs(w).max(1)
    if fmt == "e4m3":
        byte = np.frexp(amax)[1] - 1 + 127 - 7
    else:
        mant, ex = np.frexp(amax / 6.0)
        byte = np.where(mant > 0.5, ex, ex - 1) + 127
    byte = np.clip(np.where(amax > 0, byte, 1), 1, 254)
    scaled = (w * np.exp2(127.0 - byte)[:, None, :]).reshape(k, n).astype(np.float32)
    by_word = np.ascontiguousarray(scaled.reshape(k // 512, 128, 4, n).transpose(0, 1, 3, 2))
    if fmt == "e4m3":
        words = by_word.astype(ml_dtypes.float8_e4m3fn).view(np.uint8)
    else:
        c = by_word.astype(ml_dtypes.float4_e2m1fn).view(np.uint8) & 0xF
        words = (c[..., 0::2] | (c[..., 1::2] << 4)).reshape(k // 512, 128, 2 * n)
    return np.ascontiguousarray(words), np.ascontiguousarray(byte.astype(np.uint8).reshape(k // 512, 16, n))


def unpack_weight(words, scales, fmt):
    g, _, n = scales.shape
    words = np.ascontiguousarray(words).reshape(g, 128, n, -1)
    if fmt == "e4m3":
        vals = words.view(ml_dtypes.float8_e4m3fn).astype(np.float64)
    else:
        nib = np.empty((g, 128, n, 4), np.uint8)
        nib[..., 0::2] = words & 0xF
        nib[..., 1::2] = words >> 4
        vals = E2M1[nib]
    vals = vals * np.repeat(np.exp2(scales.astype(np.float64) - 127.0), 8, axis=1)[..., None]
    return vals.transpose(0, 1, 3, 2).reshape(g * 512, n)


def silu(v):
    return v / (1.0 + np.exp(-v))


def bf(x):
    return np.asarray(x, np.float32).astype(ml_dtypes.bfloat16)


def planes(Y):
    r, m = Y.shape
    b = f64(bf(Y)).reshape(r // 32, 32, m)
    amax = np.abs(b).max(1)
    byte = np.clip(np.where(amax > 0, np.frexp(amax)[1] - 1 + 127 - 7, 1), 1, 254)
    codes = (b * np.exp2(127.0 - byte)[:, None, :]).reshape(r, m).astype(np.float32).astype(ml_dtypes.float8_e4m3fn).view(np.uint8)
    words = codes.reshape(r // 512, 128, 4, m).transpose(0, 1, 3, 2)
    return np.ascontiguousarray(words), np.ascontiguousarray(byte.astype(np.uint8).reshape(r // 512, 16, m))


K, L, T, N = 1024, 1024, 512, 512


def setup_inputs():
    n = np.random.standard_normal
    fk = mx_kscale(K)
    fl = mx_kscale(L)
    wap = pack_weight(n((K, N)) * 1 / np.sqrt(K) * fk[:, None], "e4m3")
    xqp = pack_weight(n((L, T)) / fl[:, None], "e2m1")
    wqp = pack_weight(n((L, N)) * 1 / np.sqrt(L) * fl[:, None], "e4m3")
    return {
        "xf": (n((K, T)) / fk[:, None]).astype(np.float32),
        "wa_words": wap[0],
        "wa_scales": wap[1],
        "xq_words": xqp[0],
        "xq_scales": xqp[1],
        "wq_words": wqp[0],
        "wq_scales": wqp[1],
    }


def reference(xf, wa_words, wa_scales, xq_words, xq_scales, wq_words, wq_scales):
    wau = unpack_weight(wa_words, wa_scales, "e4m3")
    xqu = unpack_weight(xq_words, xq_scales, "e2m1")
    wqu = unpack_weight(wq_words, wq_scales, "e4m3")
    xp = np.pad(f64(xf), ((0, 0), (1, 0)))[:, :T]
    d = f64(xf) - xp
    dq = mxq(d, 0, "e5m2")
    z = wau.T @ dq + wqu.T @ xqu
    y = silu(0.6 * z)
    words, scales = planes(y)
    return y, words, scales

@@ -1,0 +1,151 @@
+from contextlib import ExitStack
+
+import concourse.mybir as mybir
+
+K, L, T, N = 1024, 1024, 512, 512
+FLOPS = 2 * (K + L) * T * N
+
+F32 = mybir.dt.float32
+BF16 = mybir.dt.bfloat16
+I32 = mybir.dt.int32
+U8 = mybir.dt.uint8
+E4M3 = mybir.dt.float8_e4m3fn_x4
+E5M2 = mybir.dt.float8_e5m2_x4
+E2M1 = mybir.dt.float4_e2m1fn_x4
+SILU = mybir.ActivationFunctionType.Silu
+SUB = mybir.AluOpType.subtract
+
+P = 128
+PAD = 8
+HALF = T // 2
+PIECES = ((0, 256), (256, 384), (384, 512))
+
+
+def tile_mix_change_and_state_pl_kernel(tc, xf, wa_words, wa_scales, xq_words, xq_scales, wq_words, wq_scales, out_0, out_1, out_2):
+    nc = tc.nc
+    with ExitStack() as ctx:
+        sb = ctx.enter_context(tc.tile_pool(name="sb", bufs=1))
+        ps = ctx.enter_context(tc.psum_pool(name="ps", bufs=1))
+        ctx.enter_context(tc.manual_schedule())
+
+        x = sb.tile([P, 2, 4, PAD + T], F32, name="x", align_bytes=64)
+        planes = sb.tile([P, 3, 2, T], U8, name="planes", align_bytes=64)
+        wa_raw = sb.tile([P, 2, N], I32, name="wa_raw", align_bytes=64)
+        wq_raw = [sb.tile([P, N], I32, name=f"wq_raw{z}", align_bytes=64) for z in range(2)]
+        xq = sb.tile([P, 2, 2 * T], U8, name="xq", align_bytes=64)
+        wa = [sb.tile([P, N], I32, name=f"wa{z}", align_bytes=64) for z in range(2)]
+        wq = [sb.tile([P, N], I32, name=f"wq{z}", align_bytes=64) for z in range(2)]
+        wa_plane = sb.tile([P, 2, N], U8, name="wa_plane", align_bytes=64)
+        wq_plane = sb.tile([P, 2, N], U8, name="wq_plane", align_bytes=64)
+        pairs = [[sb.tile([P, 2, HALF, 2], BF16, name=f"pairs{z}{h}", align_bytes=64) for h in range(2)] for z in range(2)]
+        quads = [[sb.tile([P, HALF * 4], BF16, name=f"quads{z}{h}", align_bytes=64) for h in range(2)] for z in range(2)]
+        dq = [sb.tile([P, T], I32, name=f"dq{z}", align_bytes=64) for z in range(2)]
+        dq_plane = [sb.tile([P, T], U8, name=f"dq_plane{z}", align_bytes=64) for z in range(2)]
+        y = [sb.tile([P, 4, b - a], F32, name=f"y{a}", align_bytes=64) for a, b in PIECES]
+        yb = [sb.tile([P, b - a, 4], BF16, name=f"yb{a}", align_bytes=64) for a, b in PIECES]
+        yq = sb.tile([P, T], I32, name="yq", align_bytes=64)
+        yq_plane = sb.tile([P, T], U8, name="yq_plane", align_bytes=64)
+        acc = [ps.tile([P, T], F32, name=f"acc{r}") for r in range(4)]
+
+        xf_v = xf.rearrange("(z p j) t -> p z j t", z=2, j=4)
+        wa_v = wa_words.rearrange("z p n t -> p z (n t)").bitcast(I32)
+        wq_v = wq_words.rearrange("z p n t -> p z (n t)").bitcast(I32)
+        xq_v = xq_words.rearrange("z p b -> p z b").bitcast(I32)
+
+        def load_x(z, u):
+            nc.sync.dma_start(out=x[:, z, 2 * u : 2 * u + 2, PAD:], in_=xf_v[:, z, 2 * u : 2 * u + 2, :])
+
+        def load_plane(eng, slot, scales):
+            rows = scales.rearrange("z q c -> q z c").bitcast(I32)
+            for quad in range(4):
+                eng.dma_start(out=planes[32 * quad : 32 * quad + 4, slot, :, :].bitcast(I32), in_=rows[4 * quad : 4 * quad + 4, :, :])
+
+        def change(z, u, h):
+            now = x[:, z, 2 * u : 2 * u + 2, PAD + h * HALF : PAD + (h + 1) * HALF]
+            before = x[:, z, 2 * u : 2 * u + 2, PAD - 1 + h * HALF : PAD - 1 + (h + 1) * HALF]
+            nc.vector.tensor_tensor(out=pairs[z][h][:, u, :, :], in0=now.rearrange("p e c -> p c e"), in1=before.rearrange("p e c -> p c e"), op=SUB)
+
+        def join(z, h):
+            words = pairs[z][h][:].rearrange("p u c e -> p u (c e)").bitcast(F32)
+            nc.scalar.copy(out=quads[z][h][:].bitcast(F32).rearrange("p (c u) -> p c u", u=2), in_=words.rearrange("p u c -> p c u"))
+
+        def quantise_change(z, h):
+            cols = slice(h * HALF, (h + 1) * HALF)
+            nc.vector.quantize_mx(out=dq[z][:, cols].bitcast(E5M2), scales=dq_plane[z][:, cols], in_=quads[z][h][:])
+
+        def deal_words(dst, src):
+            nc.vector.tensor_copy(out=dst.rearrange("p (r a i) -> p a r i", r=4, i=4), in_=src.rearrange("p (a i r) -> p a r i", r=4, i=4))
+
+        def deal_plane(dst, slot):
+            nc.vector.tensor_copy(out=dst[:].rearrange("p z (r m) -> p z r m", r=4), in_=planes[:, slot, :, :].rearrange("p z (m r) -> p z r m", r=4))
+
+        def change_pass(z, r):
+            cols = slice(r * P, (r + 1) * P)
+            nc.tensor.matmul_mx(out=acc[r][:], lhsT=wa[z][:, cols].bitcast(E4M3), lhsT_scale=wa_plane[:, z, cols],
+                                rhs=dq[z][:].bitcast(E5M2), rhs_scale=dq_plane[z][:], start=(z == 0), stop=(z == 1))
+
+        def state_pass(z, r):
+            cols = slice(r * P, (r + 1) * P)
+            nc.tensor.matmul_mx(out=acc[r][:], lhsT=wq[z][:, cols].bitcast(E4M3), lhsT_scale=wq_plane[:, z, cols],
+                                rhs=xq[:, z, :].bitcast(E2M1), rhs_scale=planes[:, 2, z, :], start=False, stop=False)
+
+        nc.vector.memset(x[:, 0, :, PAD - 4 : PAD], 0.0)
+        nc.vector.memset(planes[:].rearrange("p s z c -> p (s z c)").bitcast(I32), 0)
+        nc.scalar.activation(out=x[:, 1, :, PAD - 4 : PAD], in_=x[:, 0, :, PAD - 4 : PAD], func=SILU)
+
+        load_x(0, 0)
+        load_x(0, 1)
+        load_plane(nc.sync, 0, wa_scales)
+        nc.sync.dma_start(out=wa_raw[:], in_=wa_v)
+        nc.sync.dma_start(out=wq_raw[0][:], in_=wq_v[:, 0, :])
+        nc.sync.dma_start(out=xq[:].bitcast(I32), in_=xq_v)
+        load_plane(nc.gpsimd, 1, wq_scales)
+        load_plane(nc.sync, 2, xq_scales)
+        load_x(1, 0)
+        load_x(1, 1)
+        nc.sync.dma_start(out=wq_raw[1][:], in_=wq_v[:, 1, :])
+
+        for u in range(2):
+            for h in range(2):
+                change(0, u, h)
+        join(0, 0)
+        join(0, 1)
+        deal_plane(wa_plane, 0)
+        deal_words(wa[0][:], wa_raw[:, 0, :])
+        quantise_change(0, 0)
+        quantise_change(0, 1)
+        for r in range(4):
+            change_pass(0, r)
+        deal_plane(wq_plane, 1)
+        deal_words(wq[0][:], wq_raw[0][:])
+        for r in range(4):
+            state_pass(0, r)
+        deal_words(wa[1][:], wa_raw[:, 1, :])
+        for u in range(2):
+            for h in range(2):
+                change(1, u, h)
+        join(1, 0)
+        join(1, 1)
+        deal_words(wq[1][:], wq_raw[1][:])
+        for r in range(4):
+            state_pass(1, r)
+        quantise_change(1, 0)
+        quantise_change(1, 1)
+        for r in range(4):
+            change_pass(1, r)
+
+        out_v = out_0.rearrange("(p r) t -> p r t", r=4)
+        words_v = out_1.rearrange("z p c r -> p (z c r)").bitcast(I32)
+        for n, (a, b) in enumerate(PIECES):
+            for r in range(4):
+                nc.scalar.activation(out=y[n][:, r, :], in_=acc[r][:, a:b], func=SILU, scale=0.6)
+            nc.sync.dma_start(out=out_v[:, :, a:b], in_=y[n][:])
+            nc.vector.tensor_copy(out=yb[n][:], in_=y[n][:].rearrange("p r c -> p c r"))
+            nc.vector.quantize_mx(out=yq[:, a:b].bitcast(E4M3), scales=yq_plane[:, a:b], in_=yb[n][:].rearrange("p c r -> p (c r)"))
+            if n != 1:
+                lo = 0 if n == 0 else 256
+                nc.sync.dma_start(out=words_v[:, lo:b], in_=yq[:, lo:b])
+        rows_v = out_2.rearrange("z q c -> (z q) c").bitcast(I32)
+        for quad in range(4):
+            eng = nc.scalar if quad % 2 == 0 else nc.sync
+            eng.dma_start(out=rows_v[4 * quad : 4 * quad + 4, :], in_=yq_plane[32 * quad : 32 * quad + 4, :].bitcast(I32))

@@ -12,13 +12,11 @@ U8 = mybir.dt.uint8
 E4M3 = mybir.dt.float8_e4m3fn_x4
 E5M2 = mybir.dt.float8_e5m2_x4
 E2M1 = mybir.dt.float4_e2m1fn_x4
-SILU = mybir.ActivationFunctionType.Silu
-SUB = mybir.AluOpType.subtract
 
 P = 128
 PAD = 8
 HALF = T // 2
-PIECES = ((0, 256), (256, 384), (384, 512))
+QUARTER = T // 4
 
 
 def tile_mix_change_and_state_pl_kernel(tc, xf, wa_words, wa_scales, xq_words, xq_scales, wq_words, wq_scales, out_0, out_1, out_2):
@@ -28,42 +26,56 @@ def tile_mix_change_and_state_pl_kernel(tc, xf, wa_words, wa_scales, xq_words, x
         ps = ctx.enter_context(tc.psum_pool(name="ps", bufs=1))
         ctx.enter_context(tc.manual_schedule())
 
-        x = sb.tile([P, 2, 4, PAD + T], F32, name="x", align_bytes=64)
-        planes = sb.tile([P, 3, 2, T], U8, name="planes", align_bytes=64)
-        wa_raw = sb.tile([P, 2, N], I32, name="wa_raw", align_bytes=64)
-        wq_raw = [sb.tile([P, N], I32, name=f"wq_raw{z}", align_bytes=64) for z in range(2)]
-        xq = sb.tile([P, 2, 2 * T], U8, name="xq", align_bytes=64)
-        wa = [sb.tile([P, N], I32, name=f"wa{z}", align_bytes=64) for z in range(2)]
-        wq = [sb.tile([P, N], I32, name=f"wq{z}", align_bytes=64) for z in range(2)]
-        wa_plane = sb.tile([P, 2, N], U8, name="wa_plane", align_bytes=64)
-        wq_plane = sb.tile([P, 2, N], U8, name="wq_plane", align_bytes=64)
-        pairs = [[sb.tile([P, 2, HALF, 2], BF16, name=f"pairs{z}{h}", align_bytes=64) for h in range(2)] for z in range(2)]
-        quads = [[sb.tile([P, HALF * 4], BF16, name=f"quads{z}{h}", align_bytes=64) for h in range(2)] for z in range(2)]
-        dq = [sb.tile([P, T], I32, name=f"dq{z}", align_bytes=64) for z in range(2)]
-        dq_plane = [sb.tile([P, T], U8, name=f"dq_plane{z}", align_bytes=64) for z in range(2)]
-        y = [sb.tile([P, 4, b - a], F32, name=f"y{a}", align_bytes=64) for a, b in PIECES]
-        yb = [sb.tile([P, b - a, 4], BF16, name=f"yb{a}", align_bytes=64) for a, b in PIECES]
-        yq = sb.tile([P, T], I32, name="yq", align_bytes=64)
-        yq_plane = sb.tile([P, T], U8, name="yq_plane", align_bytes=64)
+        def tiles(name, count, shape, dtype):
+            return [sb.tile(shape, dtype, name=f"{name}{i}", align_bytes=64) for i in range(count)]
+
+        x = [tiles(f"x{z}", 2, [P, 2, PAD + T], F32) for z in range(2)]
+        pairs = [tiles(f"pairs{z}", 2, [P, 2, HALF, 2], BF16) for z in range(2)]
+        quads = [tiles(f"quads{z}", 2, [P, 4 * HALF], BF16) for z in range(2)]
+        d_codes = tiles("d_codes", 2, [P, T], I32)
+        d_scales = tiles("d_scales", 2, [P, T], U8)
+        wa_raw = tiles("wa_raw", 2, [P, N], I32)
+        wq_raw = tiles("wq_raw", 2, [P, N], I32)
+        wa_codes = tiles("wa_codes", 2, [P, N], I32)
+        wq_codes = tiles("wq_codes", 2, [P, N], I32)
+        xq_codes = tiles("xq_codes", 2, [P, 2 * T], U8)
+        wa_raw_scales, wq_raw_scales, wq_dealt_scales, xq_scale_rows = tiles("scales", 4, [P, 2, T], U8)
+        wa_dealt_scales = tiles("wa_dealt_scales", 2, [P, 1, N], U8)
+        y = tiles("y", 2, [P, 4, HALF], F32)
+        y_first = sb.tile([P, HALF, 4], BF16, align_bytes=64)
+        y_third, y_fourth = tiles("y_quarter", 2, [P, QUARTER, 4], BF16)
+        y_codes = sb.tile([P, T], I32, align_bytes=64)
+        y_scales = sb.tile([P, T], U8, align_bytes=64)
         acc = [ps.tile([P, T], F32, name=f"acc{r}") for r in range(4)]
 
         xf_v = xf.rearrange("(z p j) t -> p z j t", z=2, j=4)
-        wa_v = wa_words.rearrange("z p n t -> p z (n t)").bitcast(I32)
-        wq_v = wq_words.rearrange("z p n t -> p z (n t)").bitcast(I32)
-        xq_v = xq_words.rearrange("z p b -> p z b").bitcast(I32)
+        out_v = out_0.rearrange("(p r) t -> p r t", r=4)
+        codes_v = out_1.rearrange("z p c r -> p (z c r)").bitcast(I32)
+        scales_v = out_2.rearrange("z q c -> (z q) c").bitcast(I32)
 
         def load_x(z, u):
-            nc.sync.dma_start(out=x[:, z, 2 * u : 2 * u + 2, PAD:], in_=xf_v[:, z, 2 * u : 2 * u + 2, :])
+            nc.sync.dma_start(out=x[z][u][:, :, PAD:], in_=xf_v[:, z, 2 * u : 2 * u + 2, :])
 
-        def load_plane(eng, slot, scales):
+        def load_weights(dst, words, z):
+            nc.sync.dma_start(out=dst[z][:], in_=words[z].rearrange("p n j -> p (n j)").bitcast(I32))
+
+        def load_state(z):
+            nc.sync.dma_start(out=xq_codes[z][:].bitcast(I32), in_=xq_words[z].bitcast(I32))
+
+        def load_scales(dst, scales):
             rows = scales.rearrange("z q c -> q z c").bitcast(I32)
-            for quad in range(4):
-                eng.dma_start(out=planes[32 * quad : 32 * quad + 4, slot, :, :].bitcast(I32), in_=rows[4 * quad : 4 * quad + 4, :, :])
+            for s in range(4):
+                nc.sync.dma_start(out=dst[s:P:32, :, :].bitcast(I32), in_=rows[s:16:4, :, :])
 
         def change(z, u, h):
-            now = x[:, z, 2 * u : 2 * u + 2, PAD + h * HALF : PAD + (h + 1) * HALF]
-            before = x[:, z, 2 * u : 2 * u + 2, PAD - 1 + h * HALF : PAD - 1 + (h + 1) * HALF]
-            nc.vector.tensor_tensor(out=pairs[z][h][:, u, :, :], in0=now.rearrange("p e c -> p c e"), in1=before.rearrange("p e c -> p c e"), op=SUB)
+            now = x[z][u][:, :, PAD + h * HALF : PAD + (h + 1) * HALF]
+            before = x[z][u][:, :, PAD - 1 + h * HALF : PAD - 1 + (h + 1) * HALF]
+            nc.vector.tensor_tensor(
+                out=pairs[z][h][:, u, :, :].rearrange("p (a i) e -> p a e i", i=4),
+                in0=now.rearrange("p e (a i) -> p a e i", i=4),
+                in1=before.rearrange("p e (a i) -> p a e i", i=4),
+                op=mybir.AluOpType.subtract,
+            )
 
         def join(z, h):
             words = pairs[z][h][:].rearrange("p u c e -> p u (c e)").bitcast(F32)
@@ -71,81 +83,107 @@ def tile_mix_change_and_state_pl_kernel(tc, xf, wa_words, wa_scales, xq_words, x
 
         def quantise_change(z, h):
             cols = slice(h * HALF, (h + 1) * HALF)
-            nc.vector.quantize_mx(out=dq[z][:, cols].bitcast(E5M2), scales=dq_plane[z][:, cols], in_=quads[z][h][:])
+            nc.vector.quantize_mx(out=d_codes[z][:, cols].bitcast(E5M2), scales=d_scales[z][:, cols], in_=quads[z][h][:])
 
-        def deal_words(dst, src):
-            nc.vector.tensor_copy(out=dst.rearrange("p (r a i) -> p a r i", r=4, i=4), in_=src.rearrange("p (a i r) -> p a r i", r=4, i=4))
+        def deal_codes(dst, src):
+            nc.vector.tensor_copy(out=dst[:].rearrange("p (r a i) -> p a r i", r=4, i=4), in_=src[:].rearrange("p (a i r) -> p a r i", r=4, i=4))
 
-        def deal_plane(dst, slot):
-            nc.vector.tensor_copy(out=dst[:].rearrange("p z (r m) -> p z r m", r=4), in_=planes[:, slot, :, :].rearrange("p z (m r) -> p z r m", r=4))
+        def deal_scales(dst, src):
+            nc.vector.tensor_copy(out=dst[:].rearrange("p z (r m) -> p z r m", r=4), in_=src.rearrange("p z (m r) -> p z r m", r=4))
 
-        def change_pass(z, r):
-            cols = slice(r * P, (r + 1) * P)
-            nc.tensor.matmul_mx(out=acc[r][:], lhsT=wa[z][:, cols].bitcast(E4M3), lhsT_scale=wa_plane[:, z, cols],
-                                rhs=dq[z][:].bitcast(E5M2), rhs_scale=dq_plane[z][:], start=(z == 0), stop=(z == 1))
+        def change_passes(z):
+            for r in range(4):
+                cols = slice(r * P, (r + 1) * P)
+                nc.tensor.matmul_mx(out=acc[r][:], lhsT=wa_codes[z][:, cols].bitcast(E4M3), lhsT_scale=wa_dealt_scales[z][:, 0, cols],
+                                    rhs=d_codes[z][:].bitcast(E5M2), rhs_scale=d_scales[z][:], start=(z == 0), stop=(z == 1))
 
-        def state_pass(z, r):
-            cols = slice(r * P, (r + 1) * P)
-            nc.tensor.matmul_mx(out=acc[r][:], lhsT=wq[z][:, cols].bitcast(E4M3), lhsT_scale=wq_plane[:, z, cols],
-                                rhs=xq[:, z, :].bitcast(E2M1), rhs_scale=planes[:, 2, z, :], start=False, stop=False)
+        def state_passes(z):
+            for r in range(4):
+                cols = slice(r * P, (r + 1) * P)
+                nc.tensor.matmul_mx(out=acc[r][:], lhsT=wq_codes[z][:, cols].bitcast(E4M3), lhsT_scale=wq_dealt_scales[:, z, cols],
+                                    rhs=xq_codes[z][:].bitcast(E2M1), rhs_scale=xq_scale_rows[:, z, :], start=False, stop=False)
 
-        nc.vector.memset(x[:, 0, :, PAD - 4 : PAD], 0.0)
-        nc.vector.memset(planes[:].rearrange("p s z c -> p (s z c)").bitcast(I32), 0)
-        nc.scalar.activation(out=x[:, 1, :, PAD - 4 : PAD], in_=x[:, 0, :, PAD - 4 : PAD], func=SILU)
+        def activate(h, rows, first, width):
+            for r in rows:
+                nc.scalar.activation(out=y[h][:, r, first : first + width], in_=acc[r][:, h * HALF + first : h * HALF + first + width],
+                                     func=mybir.ActivationFunctionType.Silu, scale=0.6)
+
+        def store_rows(h, r):
+            nc.sync.dma_start(out=out_v[:, r : r + 2, h * HALF : (h + 1) * HALF], in_=y[h][:, r : r + 2, :])
+
+        def round_result(dst, src):
+            nc.vector.tensor_copy(out=dst[:].rearrange("p (a i) r -> p a r i", i=4), in_=src.rearrange("p r (a i) -> p a r i", i=4))
+
+        def quantise_result(src, first, width):
+            cols = slice(first, first + width)
+            nc.vector.quantize_mx(out=y_codes[:, cols].bitcast(E4M3), scales=y_scales[:, cols], in_=src[:].rearrange("p c r -> p (c r)"))
+
+        for scales in (wa_raw_scales, wq_raw_scales, xq_scale_rows):
+            nc.vector.memset(scales[:].rearrange("p z c -> p (z c)").bitcast(I32), 0)
+        for u in range(2):
+            nc.gpsimd.memset(x[0][u][:, :, PAD - 4 : PAD], 0.0)
+            nc.scalar.activation(out=x[1][u][:, :, PAD - 4 : PAD], in_=x[0][u][:, :, PAD - 4 : PAD], func=mybir.ActivationFunctionType.Silu)
 
         load_x(0, 0)
         load_x(0, 1)
-        load_plane(nc.sync, 0, wa_scales)
-        nc.sync.dma_start(out=wa_raw[:], in_=wa_v)
-        nc.sync.dma_start(out=wq_raw[0][:], in_=wq_v[:, 0, :])
-        nc.sync.dma_start(out=xq[:].bitcast(I32), in_=xq_v)
-        load_plane(nc.gpsimd, 1, wq_scales)
-        load_plane(nc.sync, 2, xq_scales)
+        load_weights(wa_raw, wa_words, 0)
+        load_scales(wa_raw_scales, wa_scales)
         load_x(1, 0)
+        load_weights(wq_raw, wq_words, 0)
+        load_scales(wq_raw_scales, wq_scales)
         load_x(1, 1)
-        nc.sync.dma_start(out=wq_raw[1][:], in_=wq_v[:, 1, :])
+        load_state(0)
+        load_scales(xq_scale_rows, xq_scales)
+        load_weights(wq_raw, wq_words, 1)
+        load_state(1)
+        load_weights(wa_raw, wa_words, 1)
 
-        for u in range(2):
-            for h in range(2):
-                change(0, u, h)
+        change(0, 0, 0)
+        change(0, 0, 1)
+        change(0, 1, 0)
         join(0, 0)
+        change(0, 1, 1)
         join(0, 1)
-        deal_plane(wa_plane, 0)
-        deal_words(wa[0][:], wa_raw[:, 0, :])
+        deal_codes(wa_codes[0], wa_raw[0])
         quantise_change(0, 0)
+        deal_scales(wa_dealt_scales[0], wa_raw_scales[:, 0:1, :])
         quantise_change(0, 1)
-        for r in range(4):
-            change_pass(0, r)
-        deal_plane(wq_plane, 1)
-        deal_words(wq[0][:], wq_raw[0][:])
-        for r in range(4):
-            state_pass(0, r)
-        deal_words(wa[1][:], wa_raw[:, 1, :])
-        for u in range(2):
-            for h in range(2):
-                change(1, u, h)
+        change_passes(0)
+        deal_scales(wa_dealt_scales[1], wa_raw_scales[:, 1:2, :])
+
+        change(1, 0, 0)
+        change(1, 0, 1)
+        deal_codes(wq_codes[0], wq_raw[0])
+        deal_scales(wq_dealt_scales, wq_raw_scales[:])
+        state_passes(0)
+        change(1, 1, 0)
         join(1, 0)
+        change(1, 1, 1)
         join(1, 1)
-        deal_words(wq[1][:], wq_raw[1][:])
-        for r in range(4):
-            state_pass(1, r)
+        deal_codes(wq_codes[1], wq_raw[1])
+        state_passes(1)
         quantise_change(1, 0)
         quantise_change(1, 1)
-        for r in range(4):
-            change_pass(1, r)
+        deal_codes(wa_codes[1], wa_raw[1])
+        change_passes(1)
 
-        out_v = out_0.rearrange("(p r) t -> p r t", r=4)
-        words_v = out_1.rearrange("z p c r -> p (z c r)").bitcast(I32)
-        for n, (a, b) in enumerate(PIECES):
-            for r in range(4):
-                nc.scalar.activation(out=y[n][:, r, :], in_=acc[r][:, a:b], func=SILU, scale=0.6)
-            nc.sync.dma_start(out=out_v[:, :, a:b], in_=y[n][:])
-            nc.vector.tensor_copy(out=yb[n][:], in_=y[n][:].rearrange("p r c -> p c r"))
-            nc.vector.quantize_mx(out=yq[:, a:b].bitcast(E4M3), scales=yq_plane[:, a:b], in_=yb[n][:].rearrange("p c r -> p (c r)"))
-            if n != 1:
-                lo = 0 if n == 0 else 256
-                nc.sync.dma_start(out=words_v[:, lo:b], in_=yq[:, lo:b])
-        rows_v = out_2.rearrange("z q c -> (z q) c").bitcast(I32)
-        for quad in range(4):
-            eng = nc.scalar if quad % 2 == 0 else nc.sync
-            eng.dma_start(out=rows_v[4 * quad : 4 * quad + 4, :], in_=yq_plane[32 * quad : 32 * quad + 4, :].bitcast(I32))
+        activate(0, (0, 1), 0, HALF)
+        store_rows(0, 0)
+        activate(0, (2, 3), 0, HALF)
+        store_rows(0, 2)
+        round_result(y_first, y[0][:])
+        activate(1, (0, 1), 0, HALF)
+        store_rows(1, 0)
+        activate(1, (2, 3), 0, QUARTER)
+        round_result(y_third, y[1][:, :, :QUARTER])
+        activate(1, (2, 3), QUARTER, QUARTER)
+        store_rows(1, 2)
+        nc.scalar.copy(out=y_fourth[:], in_=y[1][:, :, QUARTER:].rearrange("p r c -> p c r"))
+        quantise_result(y_first, 0, HALF)
+        nc.sync.dma_start(out=codes_v[:, :HALF], in_=y_codes[:, :HALF])
+        quantise_result(y_third, HALF, QUARTER)
+        quantise_result(y_fourth, HALF + QUARTER, QUARTER)
+        nc.scalar.dma_start(out=codes_v[:, HALF:], in_=y_codes[:, HALF:])
+        for s in range(4):
+            queue = nc.scalar if s == 3 else nc.sync
+            queue.dma_start(out=scales_v[s:16:4, :], in_=y_scales[s:P:32, :].bitcast(I32))

from contextlib import ExitStack

import concourse.mybir as mybir

K, L, T, N = 1024, 1024, 512, 512
FLOPS = 2 * (K + L) * T * N

F32 = mybir.dt.float32
BF16 = mybir.dt.bfloat16
I32 = mybir.dt.int32
U8 = mybir.dt.uint8
E4M3 = mybir.dt.float8_e4m3fn_x4
E5M2 = mybir.dt.float8_e5m2_x4
E2M1 = mybir.dt.float4_e2m1fn_x4

P = 128
PAD = 8
HALF = T // 2
QUARTER = T // 4


def tile_mix_change_and_state_pl_kernel(tc, xf, wa_words, wa_scales, xq_words, xq_scales, wq_words, wq_scales, out_0, out_1, out_2):
    nc = tc.nc
    with ExitStack() as ctx:
        sb = ctx.enter_context(tc.tile_pool(name="sb", bufs=1))
        ps = ctx.enter_context(tc.psum_pool(name="ps", bufs=1))
        ctx.enter_context(tc.manual_schedule())

        def tiles(name, count, shape, dtype):
            return [sb.tile(shape, dtype, name=f"{name}{i}", align_bytes=64) for i in range(count)]

        x = [tiles(f"x{z}", 2, [P, 2, PAD + T], F32) for z in range(2)]
        pairs = [tiles(f"pairs{z}", 2, [P, 2, HALF, 2], BF16) for z in range(2)]
        quads = [tiles(f"quads{z}", 2, [P, 4 * HALF], BF16) for z in range(2)]
        d_codes = tiles("d_codes", 2, [P, T], I32)
        d_scales = tiles("d_scales", 2, [P, T], U8)
        wa_raw = tiles("wa_raw", 2, [P, N], I32)
        wq_raw = tiles("wq_raw", 2, [P, N], I32)
        wa_codes = tiles("wa_codes", 2, [P, N], I32)
        wq_codes = tiles("wq_codes", 2, [P, N], I32)
        xq_codes = tiles("xq_codes", 2, [P, 2 * T], U8)
        wa_raw_scales, wq_raw_scales, wq_dealt_scales, xq_scale_rows = tiles("scales", 4, [P, 2, T], U8)
        wa_dealt_scales = tiles("wa_dealt_scales", 2, [P, 1, N], U8)
        y = tiles("y", 2, [P, 4, HALF], F32)
        y_first = sb.tile([P, HALF, 4], BF16, align_bytes=64)
        y_third, y_fourth = tiles("y_quarter", 2, [P, QUARTER, 4], BF16)
        y_codes = sb.tile([P, T], I32, align_bytes=64)
        y_scales = sb.tile([P, T], U8, align_bytes=64)
        acc = [ps.tile([P, T], F32, name=f"acc{r}") for r in range(4)]

        xf_v = xf.rearrange("(z p j) t -> p z j t", z=2, j=4)
        out_v = out_0.rearrange("(p r) t -> p r t", r=4)
        codes_v = out_1.rearrange("z p c r -> p (z c r)").bitcast(I32)
        scales_v = out_2.rearrange("z q c -> (z q) c").bitcast(I32)

        def load_x(z, u):
            nc.sync.dma_start(out=x[z][u][:, :, PAD:], in_=xf_v[:, z, 2 * u : 2 * u + 2, :])

        def load_weights(dst, words, z):
            nc.sync.dma_start(out=dst[z][:], in_=words[z].rearrange("p n j -> p (n j)").bitcast(I32))

        def load_state(z):
            nc.sync.dma_start(out=xq_codes[z][:].bitcast(I32), in_=xq_words[z].bitcast(I32))

        def load_scales(dst, scales):
            rows = scales.rearrange("z q c -> q z c").bitcast(I32)
            for s in range(4):
                nc.sync.dma_start(out=dst[s:P:32, :, :].bitcast(I32), in_=rows[s:16:4, :, :])

        def change(z, u, h):
            now = x[z][u][:, :, PAD + h * HALF : PAD + (h + 1) * HALF]
            before = x[z][u][:, :, PAD - 1 + h * HALF : PAD - 1 + (h + 1) * HALF]
            nc.vector.tensor_tensor(
                out=pairs[z][h][:, u, :, :].rearrange("p (a i) e -> p a e i", i=4),
                in0=now.rearrange("p e (a i) -> p a e i", i=4),
                in1=before.rearrange("p e (a i) -> p a e i", i=4),
                op=mybir.AluOpType.subtract,
            )

        def join(z, h):
            words = pairs[z][h][:].rearrange("p u c e -> p u (c e)").bitcast(F32)
            nc.scalar.copy(out=quads[z][h][:].bitcast(F32).rearrange("p (c u) -> p c u", u=2), in_=words.rearrange("p u c -> p c u"))

        def quantise_change(z, h):
            cols = slice(h * HALF, (h + 1) * HALF)
            nc.vector.quantize_mx(out=d_codes[z][:, cols].bitcast(E5M2), scales=d_scales[z][:, cols], in_=quads[z][h][:])

        def deal_codes(dst, src):
            nc.vector.tensor_copy(out=dst[:].rearrange("p (r a i) -> p a r i", r=4, i=4), in_=src[:].rearrange("p (a i r) -> p a r i", r=4, i=4))

        def deal_scales(dst, src):
            nc.vector.tensor_copy(out=dst[:].rearrange("p z (r m) -> p z r m", r=4), in_=src.rearrange("p z (m r) -> p z r m", r=4))

        def change_passes(z):
            for r in range(4):
                cols = slice(r * P, (r + 1) * P)
                nc.tensor.matmul_mx(out=acc[r][:], lhsT=wa_codes[z][:, cols].bitcast(E4M3), lhsT_scale=wa_dealt_scales[z][:, 0, cols],
                                    rhs=d_codes[z][:].bitcast(E5M2), rhs_scale=d_scales[z][:], start=(z == 0), stop=(z == 1))

        def state_passes(z):
            for r in range(4):
                cols = slice(r * P, (r + 1) * P)
                nc.tensor.matmul_mx(out=acc[r][:], lhsT=wq_codes[z][:, cols].bitcast(E4M3), lhsT_scale=wq_dealt_scales[:, z, cols],
                                    rhs=xq_codes[z][:].bitcast(E2M1), rhs_scale=xq_scale_rows[:, z, :], start=False, stop=False)

        def activate(h, rows, first, width):
            for r in rows:
                nc.scalar.activation(out=y[h][:, r, first : first + width], in_=acc[r][:, h * HALF + first : h * HALF + first + width],
                                     func=mybir.ActivationFunctionType.Silu, scale=0.6)

        def store_rows(h, r):
            nc.sync.dma_start(out=out_v[:, r : r + 2, h * HALF : (h + 1) * HALF], in_=y[h][:, r : r + 2, :])

        def round_result(dst, src):
            nc.vector.tensor_copy(out=dst[:].rearrange("p (a i) r -> p a r i", i=4), in_=src.rearrange("p r (a i) -> p a r i", i=4))

        def quantise_result(src, first, width):
            cols = slice(first, first + width)
            nc.vector.quantize_mx(out=y_codes[:, cols].bitcast(E4M3), scales=y_scales[:, cols], in_=src[:].rearrange("p c r -> p (c r)"))

        for scales in (wa_raw_scales, wq_raw_scales, xq_scale_rows):
            nc.vector.memset(scales[:].rearrange("p z c -> p (z c)").bitcast(I32), 0)
        for u in range(2):
            nc.gpsimd.memset(x[0][u][:, :, PAD - 4 : PAD], 0.0)
            nc.scalar.activation(out=x[1][u][:, :, PAD - 4 : PAD], in_=x[0][u][:, :, PAD - 4 : PAD], func=mybir.ActivationFunctionType.Silu)

        load_x(0, 0)
        load_x(0, 1)
        load_weights(wa_raw, wa_words, 0)
        load_scales(wa_raw_scales, wa_scales)
        load_x(1, 0)
        load_weights(wq_raw, wq_words, 0)
        load_scales(wq_raw_scales, wq_scales)
        load_x(1, 1)
        load_state(0)
        load_scales(xq_scale_rows, xq_scales)
        load_weights(wq_raw, wq_words, 1)
        load_state(1)
        load_weights(wa_raw, wa_words, 1)

        change(0, 0, 0)
        change(0, 0, 1)
        change(0, 1, 0)
        join(0, 0)
        change(0, 1, 1)
        join(0, 1)
        deal_codes(wa_codes[0], wa_raw[0])
        quantise_change(0, 0)
        deal_scales(wa_dealt_scales[0], wa_raw_scales[:, 0:1, :])
        quantise_change(0, 1)
        change_passes(0)
        deal_scales(wa_dealt_scales[1], wa_raw_scales[:, 1:2, :])

        change(1, 0, 0)
        change(1, 0, 1)
        deal_codes(wq_codes[0], wq_raw[0])
        deal_scales(wq_dealt_scales, wq_raw_scales[:])
        state_passes(0)
        change(1, 1, 0)
        join(1, 0)
        change(1, 1, 1)
        join(1, 1)
        deal_codes(wq_codes[1], wq_raw[1])
        state_passes(1)
        quantise_change(1, 0)
        quantise_change(1, 1)
        deal_codes(wa_codes[1], wa_raw[1])
        change_passes(1)

        activate(0, (0, 1), 0, HALF)
        store_rows(0, 0)
        activate(0, (2, 3), 0, HALF)
        store_rows(0, 2)
        round_result(y_first, y[0][:])
        activate(1, (0, 1), 0, HALF)
        store_rows(1, 0)
        activate(1, (2, 3), 0, QUARTER)
        round_result(y_third, y[1][:, :, :QUARTER])
        activate(1, (2, 3), QUARTER, QUARTER)
        store_rows(1, 2)
        nc.scalar.copy(out=y_fourth[:], in_=y[1][:, :, QUARTER:].rearrange("p r c -> p c r"))
        quantise_result(y_first, 0, HALF)
        nc.sync.dma_start(out=codes_v[:, :HALF], in_=y_codes[:, :HALF])
        quantise_result(y_third, HALF, QUARTER)
        quantise_result(y_fourth, HALF + QUARTER, QUARTER)
        nc.scalar.dma_start(out=codes_v[:, HALF:], in_=y_codes[:, HALF:])
        for s in range(4):
            queue = nc.scalar if s == 3 else nc.sync
            queue.dma_start(out=scales_v[s:16:4, :], in_=y_scales[s:P:32, :].bitcast(I32))
